import numpy as np
import ml_dtypes


def mxq(x, axis, fmt="e4m3"):
    dtype, down = {"e4m3": (ml_dtypes.float8_e4m3fn, 7), "e5m2": (ml_dtypes.float8_e5m2, 14)}[fmt]
    v = np.moveaxis(np.asarray(x, np.float32).astype(ml_dtypes.bfloat16).astype(np.float64), axis, -1)
    blocks = v.reshape(v.shape[:-1] + (-1, 32))
    amax = np.abs(blocks).max(-1, keepdims=True)
    byte = np.maximum(np.where(amax > 0, np.frexp(amax)[1] - 1 + 127, 0) - down, 1)
    scale = np.exp2(byte - 127.0)
    codes = (blocks / scale).astype(np.float32).astype(dtype).astype(np.float64)
    return np.moveaxis((codes * scale).reshape(v.shape), -1, axis)


WIDE = False


def mx_kscale(k):
    if not WIDE:
        return np.ones(k)
    levels = np.array([10, -10, 5, -5, 0])
    if k % 512:
        return np.exp2(np.random.permutation(np.resize(levels, k // 32))).repeat(32)
    a = np.empty((k // 512, 16))
    for p in range(k // 512):
        a[p, :8] = np.random.permutation(np.resize(levels, 8))
        for g in range(8):
            far = levels[np.abs(levels - a[p, g]) >= 10]
            a[p, g + 8] = far[np.random.randint(len(far))]
    return np.exp2(a.ravel()).repeat(32)


def f64(x):
    return np.asarray(x).astype(np.float64)


def striped(idx):
    return np.tile(np.asarray(idx).reshape(-1, 16).T, (8, 1)).astype(np.uint16)


def unstriped(offs):
    return offs[:16].T.reshape(-1).astype(np.int64)


E2M1 = np.array([0.0, 0.5, 1.0, 1.5, 2.0, 3.0, 4.0, 6.0, -0.0, -0.5, -1.0, -1.5, -2.0, -3.0, -4.0, -6.0])


def pack_weight(w, fmt):
    k, n = w.shape
    w = f64(np.asarray(w, np.float32).astype(ml_dtypes.bfloat16)).reshape(k // 32, 32, n)
    amax = np.abs(w).max(1)
    if fmt == "e4m3":
        byte = np.frexp(amax)[1] - 1 + 127 - 7
    else:
        mant, ex = np.frexp(amax / 6.0)
        byte = np.where(mant > 0.5, ex, ex - 1) + 127
    byte = np.clip(np.where(amax > 0, byte, 1), 1, 254)
    scaled = (w * np.exp2(127.0 - byte)[:, None, :]).reshape(k, n).astype(np.float32)
    by_word = np.ascontiguousarray(scaled.reshape(k // 512, 128, 4, n).transpose(0, 1, 3, 2))
    if fmt == "e4m3":
        words = by_word.astype(ml_dtypes.float8_e4m3fn).view(np.uint8)
    else:
        c = by_word.astype(ml_dtypes.float4_e2m1fn).view(np.uint8) & 0xF
        words = (c[..., 0::2] | (c[..., 1::2] << 4)).reshape(k // 512, 128, 2 * n)
    return np.ascontiguousarray(words), np.ascontiguousarray(byte.astype(np.uint8).reshape(k // 512, 16, n))


def unpack_weight(words, scales, fmt):
    g, _, n = scales.shape
    words = np.ascontiguousarray(words).reshape(g, 128, n, -1)
    if fmt == "e4m3":
        vals = words.view(ml_dtypes.float8_e4m3fn).astype(np.float64)
    else:
        nib = np.empty((g, 128, n, 4), np.uint8)
        nib[..., 0::2] = words & 0xF
        nib[..., 1::2] = words >> 4
        vals = E2M1[nib]
    vals = vals * np.repeat(np.exp2(scales.astype(np.float64) - 127.0), 8, axis=1)[..., None]
    return vals.transpose(0, 1, 3, 2).reshape(g * 512, n)


def sigmoid(v):
    return 1.0 / (1.0 + np.exp(-v))


D, K, R, T, I, Q, U = 512, 512, 512, 2048, 512, 128, 1024


def setup_inputs():
    n = np.random.standard_normal
    idx2 = np.random.permutation(U)[:I]
    idx = np.random.permutation(T)[:I]
    fd = mx_kscale(D)
    fk = mx_kscale(K)
    fr = mx_kscale(R)
    keysp = pack_weight(n((D, T)) / fd[:, None], "e2m1")
    tabp = pack_weight(n((K, T)) / fk[:, None], "e2m1")
    return {
        "query": (n((D, Q)) * 0.6 / np.sqrt(D) * fd[:, None]).astype(np.float32),
        "query2": (n((D, Q)) * 1.0 / np.sqrt(D) * fd[:, None]).astype(np.float32),
        "keys_words": keysp[0],
        "keys_scales": keysp[1],
        "tab_words": tabp[0],
        "tab_scales": tabp[1],
        "w1": (n((K, R)) * 1 / np.sqrt(K) * fk[:, None]).astype(np.float32),
        "gtab": (n((R, U))).astype(np.float32),
        "gout": (n((R, Q)) * 1 / np.sqrt(R) * fr[:, None]).astype(np.float32),
        "hsc": (np.random.uniform(0.7, 1.4, (R, 1)) / fr[:, None]).astype(np.float32),
        "old": (0.5 * n((Q, T))).astype(np.float32),
        "offs2": striped(idx2),
        "offs": striped(idx),
    }


def reference(query, query2, keys_words, keys_scales, tab_words, tab_scales, w1, gtab, gout, hsc, old, offs2, offs):
    idx2 = unstriped(offs2)
    idx = unstriped(offs)
    keysu = unpack_weight(keys_words, keys_scales, "e2m1")
    tabu = unpack_weight(tab_words, tab_scales, "e2m1")
    queryq = mxq(f64(query), 0, "e4m3")
    keysidxg = keysu[:, idx]
    a = queryq.T @ keysidxg
    query2q = mxq(f64(query2), 0, "e4m3")
    b = query2q.T @ keysidxg
    p = np.exp(a - np.max(a, axis=1, keepdims=True)) * sigmoid(b)
    z = np.sum(p, axis=1, keepdims=True)
    w1q = mxq(f64(w1), 0, "e4m3")
    tabidxg = tabu[:, idx]
    zh = w1q.T @ tabidxg
    hg = sigmoid(f64(gtab)[:, idx2])
    hv = zh * hg
    hs1 = hv * f64(hsc)
    goutq = mxq(f64(gout), 0, "e4m3")
    hs1q = mxq(hs1, 0, "e4m3")
    c0 = goutq.T @ hs1q
    dz = np.sum(c0 * p / np.square(z) * (-1.0), axis=1, keepdims=True)
    dp = c0 / z + dz
    da = dp * sigmoid(b) * np.exp(a - np.max(a, axis=1, keepdims=True))
    gs = da * 512.0
    gf = np.zeros((Q, T))
    gf[:, idx] = gs
    y = f64(old) + gf
    return y

@@ -1,0 +1,194 @@
+from contextlib import ExitStack
+
+import concourse.mybir as mybir
+
+F32 = mybir.dt.float32
+BF16 = mybir.dt.bfloat16
+I32 = mybir.dt.int32
+U32 = mybir.dt.uint32
+U16 = mybir.dt.uint16
+U8 = mybir.dt.uint8
+FP8X4 = mybir.dt.float8_e4m3fn_x4
+FP4X4 = mybir.dt.float4_e2m1fn_x4
+ACT = mybir.ActivationFunctionType
+ALU = mybir.AluOpType
+AX = mybir.AxisListType
+
+P = 128
+PACK = 4
+T, U, SLOTS, Q, R = 2048, 1024, 512, 128, 512
+HALF = SLOTS // 2
+OUT_CUTS = (0, 256, 768, 1280, 1792, 2048)
+FLOPS = 469762048
+
+
+def tile_attend_blrgated_asked_kernel(tc, query, query2, keys_words, keys_scales, tab_words, tab_scales,
+                                       w1, gtab, gout, hsc, old, offs2, offs, out):
+    nc = tc.nc
+    with ExitStack() as ctx:
+        sb = ctx.enter_context(tc.tile_pool(name="sb", bufs=1))
+        ps = ctx.enter_context(tc.psum_pool(name="ps", bufs=1))
+
+        def tile(name, shape, dtype):
+            return sb.tile(shape, dtype, name=name, align_bytes=64)
+
+        tok_list = sb.tile([P, SLOTS // 16], U16, name="tok_list")
+        gate_list = sb.tile([P, SLOTS // 16], U16, name="gate_list")
+        tab_w = tile("tab_w", [P, T], U16)
+        key_w = tile("key_w", [P, T], U16)
+        tab_s = tile("tab_s", [P, T], U8)
+        key_s = tile("key_s", [P, T], U8)
+        window = tile("window", [P, T], F32)
+        warm = tile("warm", [P, 1], F32)
+        warm_out = tile("warm_out", [P, 1], F32)
+
+        nc.vector.memset(tab_s[:].bitcast(I32), 0)
+        nc.vector.memset(key_s[:].bitcast(I32), 0)
+        nc.vector.memset(warm[:], 0.0)
+
+        def load_scales(queue, dst, src):
+            rows = src[0].rearrange("(g f) c -> f g c", f=4)
+            for f in range(4):
+                queue.dma_start(out=dst[f:P:32, :].bitcast(I32), in_=rows[f].bitcast(I32))
+
+        def load_rows(name, src, c0, c1):
+            raw = tile(name, [P, PACK, c1 - c0], F32)
+            nc.sync.dma_start(out=raw[:], in_=src.rearrange("(p t) c -> p t c", t=PACK)[:, :, c0:c1])
+            return raw
+
+        gate_rows = gtab.rearrange("(p j) u -> j p u", j=PACK)
+
+        def load_gates(j):
+            g = tile("gates%d" % j, [P, U], F32)
+            nc.sync.dma_start(out=g[:], in_=gate_rows[j])
+            return g
+
+        nc.sync.dma_start(tok_list[:], offs)
+        nc.sync.dma_start(out=tab_w[:].bitcast(I32), in_=tab_words[0].bitcast(I32))
+        load_scales(nc.sync, tab_s, tab_scales)
+        nc.sync.dma_start(gate_list[:], offs2)
+        gates = [load_gates(0)]
+        load_scales(nc.gpsimd, key_s, keys_scales)
+        hsc_t = tile("hsc_t", [P, PACK], F32)
+        nc.gpsimd.dma_start(out=hsc_t[:], in_=hsc.rearrange("(p j) o -> p (j o)", j=PACK))
+        nc.gpsimd.memset(window[:], 0.0)
+        w_raw = [load_rows("w_raw0", w1, 0, R // 2), load_rows("w_raw1", w1, R // 2, R)]
+        gates.append(load_gates(1))
+        nc.sync.dma_start(out=key_w[:].bitcast(I32), in_=keys_words[0].bitcast(I32))
+        gates.append(load_gates(2))
+        gates.append(load_gates(3))
+        q2_raw = load_rows("q2_raw", query2, 0, Q)
+        q_raw = load_rows("q_raw", query, 0, Q)
+        go_raw = load_rows("go_raw", gout, 0, Q)
+        old_t = tile("old_t", [P, T], F32)
+        nc.sync.dma_start(out=old_t[:], in_=old)
+
+        nc.scalar.activation(warm_out[:], warm[:], ACT.Sigmoid)
+
+        def gather(name, src, dtype):
+            dst = tile(name, [P, SLOTS], dtype)
+            nc.vector.tensor_copy(dst[:], src[:].indirect(tok_list[:]))
+            return dst
+
+        def quantise(name, src, words):
+            codes = tile(name + "_codes", [P, words], U32)
+            scales = tile(name + "_scales", [P, words], U8)
+            nc.vector.quantize_mx(out=codes[:].bitcast(FP8X4), scales=scales[:], in_=src)
+            return codes, scales
+
+        def weave(copy, name, raw):
+            cols = raw.shape[2]
+            dst = tile(name, [P, cols * PACK], BF16)
+            copy(out=dst[:].rearrange("p (c i t) -> p c t i", i=4, t=PACK),
+                 in_=raw.rearrange("p t (c i) -> p c t i", i=4))
+            return dst
+
+        def gate(j):
+            hg = tile("hg%d" % j, [P, SLOTS], F32)
+            nc.scalar.activation(hg[:], gates[j][:].indirect(gate_list[:]), ACT.Sigmoid)
+            return hg
+
+        tab_wg = gather("tab_wg", tab_w, U16)
+        tab_sg = gather("tab_sg", tab_s, U8)
+        key_sg = gather("key_sg", key_s, U8)
+        hg = [gate(0)]
+
+        w_bf = tile("w_bf", [P, R * PACK], BF16)
+        w_view = w_bf[:].rearrange("p (j m t) -> p m t j", j=PACK, t=PACK)
+        for h, copy in enumerate((nc.scalar.copy, nc.vector.tensor_copy)):
+            copy(out=w_view[:, h * 64:(h + 1) * 64], in_=w_raw[h][:].rearrange("p t (m j) -> p m t j", j=PACK))
+        w_codes, w_scales = quantise("w", w_bf[:], R)
+        zh = []
+        for j in range(PACK):
+            bank = ps.tile([P, SLOTS], F32, name="zh%d" % j)
+            nc.tensor.matmul_mx(out=bank[:], lhsT=w_codes[:, j * P:(j + 1) * P].bitcast(FP8X4),
+                                lhsT_scale=w_scales[:, j * P:(j + 1) * P],
+                                rhs=tab_wg[:].bitcast(FP4X4), rhs_scale=tab_sg[:], start=True, stop=True)
+            zh.append(bank)
+        key_wg = gather("key_wg", key_w, U16)
+
+        planes = tile("planes", [P, PACK, SLOTS], BF16)
+
+        def hidden(j):
+            nc.vector.scalar_tensor_tensor(out=planes[:, j, :], in0=zh[j][:], scalar=hsc_t[:, j:j + 1], in1=hg[j][:],
+                                           op0=ALU.mult, op1=ALU.mult)
+
+        def score(name, bf):
+            codes, scales = quantise(name, bf[:], Q)
+            bank = ps.tile([P, SLOTS], F32, name=name + "_ps")
+            nc.tensor.matmul_mx(out=bank[:], lhsT=codes[:].bitcast(FP8X4), lhsT_scale=scales[:],
+                                rhs=key_wg[:].bitcast(FP4X4), rhs_scale=key_sg[:], start=True, stop=True)
+            return bank
+
+        hg.append(gate(1))
+        hidden(0)
+        hidden(1)
+        hg.append(gate(2))
+        hg.append(gate(3))
+        q2_bf = weave(nc.vector.tensor_copy, "q2_bf", q2_raw[:])
+        hidden(2)
+        b_ps = score("b", q2_bf)
+        q_bf = weave(nc.vector.tensor_copy, "q_bf", q_raw[:])
+        sig_b = tile("sig_b", [P, SLOTS], F32)
+        nc.scalar.activation(sig_b[:], b_ps[:], ACT.Sigmoid)
+        hidden(3)
+        a_ps = score("a", q_bf)
+        neg_max = tile("neg_max", [P, 1], F32)
+        nc.vector.tensor_reduce(out=neg_max[:], in_=a_ps[:], axis=AX.X, op=ALU.max, negate=True)
+        go_bf = weave(nc.vector.tensor_copy, "go_bf", go_raw[:])
+        nc.scalar.activation(warm_out[:], hg[3][:, 0:1], ACT.Exp, bias=sig_b[:, 0:1])
+        go_codes, go_scales = quantise("go", go_bf[:], Q)
+        e = tile("e", [P, SLOTS], F32)
+        nc.scalar.activation(e[:], a_ps[:], ACT.Exp, bias=neg_max[:])
+
+        woven = [weave(nc.vector.tensor_copy, "woven%d" % h, planes[:, :, h * HALF:(h + 1) * HALF]) for h in range(2)]
+        c0 = ps.tile([P, SLOTS], F32, name="c0")
+        for h in range(2):
+            codes, scales = quantise("hs%d" % h, woven[h][:], HALF)
+            nc.tensor.matmul_mx(out=c0[:, h * HALF:(h + 1) * HALF], lhsT=go_codes[:].bitcast(FP8X4),
+                                lhsT_scale=go_scales[:], rhs=codes[:].bitcast(FP8X4), rhs_scale=scales[:],
+                                start=True, stop=True)
+
+        p = tile("p", [P, SLOTS], F32)
+        z = tile("z", [P, 1], F32)
+        nc.vector.scalar_tensor_tensor(out=p[:], in0=e[:], scalar=1.0, in1=sig_b[:], op0=ALU.mult, op1=ALU.mult,
+                                       accum_out=z[:])
+        rz = tile("rz", [P, 1], F32)
+        nc.vector.reciprocal(rz[:], z[:])
+        rz512 = tile("rz512", [P, 1], F32)
+        neg_rz = tile("neg_rz", [P, 1], F32)
+        nc.vector.tensor_scalar(out=rz512[:], in0=rz[:], scalar1=512.0, scalar2=None, op0=ALU.mult)
+        nc.vector.tensor_scalar(out=neg_rz[:], in0=rz[:], scalar1=-1.0, scalar2=None, op0=ALU.mult)
+        direct = tile("direct", [P, SLOTS], F32)
+        total = tile("total", [P, 1], F32)
+        nc.vector.scalar_tensor_tensor(out=direct[:], in0=c0[:], scalar=rz512[:], in1=p[:], op0=ALU.mult,
+                                       op1=ALU.mult, accum_out=total[:])
+        via_z = tile("via_z", [P, SLOTS], F32)
+        nc.vector.tensor_scalar(out=via_z[:], in0=p[:], scalar1=total[:], scalar2=neg_rz[:], op0=ALU.mult,
+                                op1=ALU.mult)
+        nc.vector.tensor_tensor(window[:].indirect(tok_list[:]), direct[:], via_z[:], ALU.add)
+
+        for c0_, c1_ in zip(OUT_CUTS[:-1], OUT_CUTS[1:]):
+            res = tile("res%d" % c0_, [P, c1_ - c0_], F32)
+            nc.vector.tensor_tensor(res[:], old_t[:, c0_:c1_], window[:, c0_:c1_], ALU.add)
+            nc.sync.dma_start(out=out[:, c0_:c1_], in_=res[:])

@@ -43,8 +43,9 @@ def tile_attend_blrgated_asked_kernel(tc, query, query2, keys_words, keys_scales
         warm_out = tile("warm_out", [P, 1], F32)
 
         nc.vector.memset(tab_s[:].bitcast(I32), 0)
-        nc.vector.memset(key_s[:].bitcast(I32), 0)
         nc.vector.memset(warm[:], 0.0)
+        nc.vector.memset(key_s[:].bitcast(I32), 0)
+        nc.gpsimd.memset(window[:], 0.0)
 
         def load_scales(queue, dst, src):
             rows = src[0].rearrange("(g f) c -> f g c", f=4)
@@ -63,27 +64,26 @@ def tile_attend_blrgated_asked_kernel(tc, query, query2, keys_words, keys_scales
             nc.sync.dma_start(out=g[:], in_=gate_rows[j])
             return g
 
+        nc.scalar.activation(warm_out[:], warm[:], ACT.Sigmoid)
         nc.sync.dma_start(tok_list[:], offs)
         nc.sync.dma_start(out=tab_w[:].bitcast(I32), in_=tab_words[0].bitcast(I32))
         load_scales(nc.sync, tab_s, tab_scales)
-        nc.sync.dma_start(gate_list[:], offs2)
+        w_raw = [load_rows("w_raw0", w1, 0, R // 2)]
         gates = [load_gates(0)]
-        load_scales(nc.gpsimd, key_s, keys_scales)
-        hsc_t = tile("hsc_t", [P, PACK], F32)
-        nc.gpsimd.dma_start(out=hsc_t[:], in_=hsc.rearrange("(p j) o -> p (j o)", j=PACK))
-        nc.gpsimd.memset(window[:], 0.0)
-        w_raw = [load_rows("w_raw0", w1, 0, R // 2), load_rows("w_raw1", w1, R // 2, R)]
+        nc.sync.dma_start(gate_list[:], offs2)
+        load_scales(nc.sync, key_s, keys_scales)
+        w_raw.append(load_rows("w_raw1", w1, R // 2, R))
         gates.append(load_gates(1))
         nc.sync.dma_start(out=key_w[:].bitcast(I32), in_=keys_words[0].bitcast(I32))
+        hsc_t = tile("hsc_t", [P, PACK], F32)
+        nc.sync.dma_start(out=hsc_t[:], in_=hsc.rearrange("(p j) o -> p (j o)", j=PACK))
         gates.append(load_gates(2))
-        gates.append(load_gates(3))
         q2_raw = load_rows("q2_raw", query2, 0, Q)
+        gates.append(load_gates(3))
         q_raw = load_rows("q_raw", query, 0, Q)
         go_raw = load_rows("go_raw", gout, 0, Q)
         old_t = tile("old_t", [P, T], F32)
         nc.sync.dma_start(out=old_t[:], in_=old)
-
-        nc.scalar.activation(warm_out[:], warm[:], ACT.Sigmoid)
 
         def gather(name, src, dtype):
             dst = tile(name, [P, SLOTS], dtype)
@@ -96,10 +96,8 @@ def tile_attend_blrgated_asked_kernel(tc, query, query2, keys_words, keys_scales
             nc.vector.quantize_mx(out=codes[:].bitcast(FP8X4), scales=scales[:], in_=src)
             return codes, scales
 
-        def weave(copy, name, raw):
-            cols = raw.shape[2]
-            dst = tile(name, [P, cols * PACK], BF16)
-            copy(out=dst[:].rearrange("p (c i t) -> p c t i", i=4, t=PACK),
+        def weave(copy, dst, raw):
+            copy(out=dst.rearrange("p (c i t) -> p c t i", i=4, t=PACK),
                  in_=raw.rearrange("p t (c i) -> p c t i", i=4))
             return dst
 
@@ -111,7 +109,6 @@ def tile_attend_blrgated_asked_kernel(tc, query, query2, keys_words, keys_scales
         tab_wg = gather("tab_wg", tab_w, U16)
         tab_sg = gather("tab_sg", tab_s, U8)
         key_sg = gather("key_sg", key_s, U8)
-        hg = [gate(0)]
 
         w_bf = tile("w_bf", [P, R * PACK], BF16)
         w_view = w_bf[:].rearrange("p (j m t) -> p m t j", j=PACK, t=PACK)
@@ -125,7 +122,7 @@ def tile_attend_blrgated_asked_kernel(tc, query, query2, keys_words, keys_scales
                                 lhsT_scale=w_scales[:, j * P:(j + 1) * P],
                                 rhs=tab_wg[:].bitcast(FP4X4), rhs_scale=tab_sg[:], start=True, stop=True)
             zh.append(bank)
-        key_wg = gather("key_wg", key_w, U16)
+        hg = [gate(0)]
 
         planes = tile("planes", [P, PACK, SLOTS], BF16)
 
@@ -133,46 +130,50 @@ def tile_attend_blrgated_asked_kernel(tc, query, query2, keys_words, keys_scales
             nc.vector.scalar_tensor_tensor(out=planes[:, j, :], in0=zh[j][:], scalar=hsc_t[:, j:j + 1], in1=hg[j][:],
                                            op0=ALU.mult, op1=ALU.mult)
 
-        def score(name, bf):
-            codes, scales = quantise(name, bf[:], Q)
+        def score(name, bf, key_wg):
+            codes, scales = quantise(name, bf, Q)
             bank = ps.tile([P, SLOTS], F32, name=name + "_ps")
             nc.tensor.matmul_mx(out=bank[:], lhsT=codes[:].bitcast(FP8X4), lhsT_scale=scales[:],
                                 rhs=key_wg[:].bitcast(FP4X4), rhs_scale=key_sg[:], start=True, stop=True)
             return bank
 
         hg.append(gate(1))
+        key_wg = gather("key_wg", key_w, U16)
         hidden(0)
-        hidden(1)
         hg.append(gate(2))
+        q2_bf = weave(nc.vector.tensor_copy, planes[:, 2, :], q2_raw[:])
+        hidden(1)
+        b_ps = score("b", q2_bf, key_wg)
         hg.append(gate(3))
-        q2_bf = weave(nc.vector.tensor_copy, "q2_bf", q2_raw[:])
         hidden(2)
-        b_ps = score("b", q2_bf)
-        q_bf = weave(nc.vector.tensor_copy, "q_bf", q_raw[:])
-        sig_b = tile("sig_b", [P, SLOTS], F32)
+        q_bf = weave(nc.vector.tensor_copy, planes[:, 3, :], q_raw[:])
+        go_bf = weave(nc.vector.tensor_copy, tile("go_bf", [P, Q * PACK], BF16)[:], go_raw[:])
+        a_ps = score("a", q_bf, key_wg)
+        sig_b = tile("gates3", [P, SLOTS], F32)
         nc.scalar.activation(sig_b[:], b_ps[:], ACT.Sigmoid)
         hidden(3)
-        a_ps = score("a", q_bf)
         neg_max = tile("neg_max", [P, 1], F32)
         nc.vector.tensor_reduce(out=neg_max[:], in_=a_ps[:], axis=AX.X, op=ALU.max, negate=True)
-        go_bf = weave(nc.vector.tensor_copy, "go_bf", go_raw[:])
         nc.scalar.activation(warm_out[:], hg[3][:, 0:1], ACT.Exp, bias=sig_b[:, 0:1])
-        go_codes, go_scales = quantise("go", go_bf[:], Q)
+        go_codes, go_scales = quantise("go", go_bf, Q)
         e = tile("e", [P, SLOTS], F32)
         nc.scalar.activation(e[:], a_ps[:], ACT.Exp, bias=neg_max[:])
 
-        woven = [weave(nc.vector.tensor_copy, "woven%d" % h, planes[:, :, h * HALF:(h + 1) * HALF]) for h in range(2)]
+        woven = [weave(nc.vector.tensor_copy, tile("woven%d" % h, [P, HALF * PACK], BF16)[:], planes[:, :, h * HALF:(h + 1) * HALF]) for h in range(2)]
         c0 = ps.tile([P, SLOTS], F32, name="c0")
-        for h in range(2):
-            codes, scales = quantise("hs%d" % h, woven[h][:], HALF)
+
+        def read_grad(h):
+            codes, scales = quantise("hs%d" % h, woven[h], HALF)
             nc.tensor.matmul_mx(out=c0[:, h * HALF:(h + 1) * HALF], lhsT=go_codes[:].bitcast(FP8X4),
                                 lhsT_scale=go_scales[:], rhs=codes[:].bitcast(FP8X4), rhs_scale=scales[:],
                                 start=True, stop=True)
 
-        p = tile("p", [P, SLOTS], F32)
+        read_grad(0)
+        p = tile("woven0", [P, SLOTS], F32)
         z = tile("z", [P, 1], F32)
         nc.vector.scalar_tensor_tensor(out=p[:], in0=e[:], scalar=1.0, in1=sig_b[:], op0=ALU.mult, op1=ALU.mult,
                                        accum_out=z[:])
+        read_grad(1)
         rz = tile("rz", [P, 1], F32)
         nc.vector.reciprocal(rz[:], z[:])
         rz512 = tile("rz512", [P, 1], F32)

@@ -45,7 +45,7 @@ def tile_attend_blrgated_asked_kernel(tc, query, query2, keys_words, keys_scales
         nc.vector.memset(tab_s[:].bitcast(I32), 0)
         nc.vector.memset(warm[:], 0.0)
         nc.vector.memset(key_s[:].bitcast(I32), 0)
-        nc.gpsimd.memset(window[:], 0.0)
+        nc.vector.memset(window[:], 0.0)
 
         def load_scales(queue, dst, src):
             rows = src[0].rearrange("(g f) c -> f g c", f=4)
@@ -97,8 +97,7 @@ def tile_attend_blrgated_asked_kernel(tc, query, query2, keys_words, keys_scales
             return codes, scales
 
         def weave(copy, dst, raw):
-            copy(out=dst.rearrange("p (c i t) -> p c t i", i=4, t=PACK),
-                 in_=raw.rearrange("p t (c i) -> p c t i", i=4))
+            copy(out=dst.rearrange("p (c t) -> p c t", t=PACK), in_=raw.rearrange("p t c -> p c t"))
             return dst
 
         def gate(j):
@@ -111,9 +110,9 @@ def tile_attend_blrgated_asked_kernel(tc, query, query2, keys_words, keys_scales
         key_sg = gather("key_sg", key_s, U8)
 
         w_bf = tile("w_bf", [P, R * PACK], BF16)
-        w_view = w_bf[:].rearrange("p (j m t) -> p m t j", j=PACK, t=PACK)
+        w_view = w_bf[:].rearrange("p (j m t) -> p m j t", j=PACK, t=PACK)
         for h, copy in enumerate((nc.scalar.copy, nc.vector.tensor_copy)):
-            copy(out=w_view[:, h * 64:(h + 1) * 64], in_=w_raw[h][:].rearrange("p t (m j) -> p m t j", j=PACK))
+            copy(out=w_view[:, h * 64:(h + 1) * 64], in_=w_raw[h][:].rearrange("p t (m j) -> p m j t", j=PACK))
         w_codes, w_scales = quantise("w", w_bf[:], R)
         zh = []
         for j in range(PACK):

from contextlib import ExitStack

import concourse.mybir as mybir

F32 = mybir.dt.float32
BF16 = mybir.dt.bfloat16
I32 = mybir.dt.int32
U32 = mybir.dt.uint32
U16 = mybir.dt.uint16
U8 = mybir.dt.uint8
FP8X4 = mybir.dt.float8_e4m3fn_x4
FP4X4 = mybir.dt.float4_e2m1fn_x4
ACT = mybir.ActivationFunctionType
ALU = mybir.AluOpType
AX = mybir.AxisListType

P = 128
PACK = 4
T, U, SLOTS, Q, R = 2048, 1024, 512, 128, 512
HALF = SLOTS // 2
OUT_CUTS = (0, 256, 768, 1280, 1792, 2048)
FLOPS = 469762048


def tile_attend_blrgated_asked_kernel(tc, query, query2, keys_words, keys_scales, tab_words, tab_scales,
                                       w1, gtab, gout, hsc, old, offs2, offs, out):
    nc = tc.nc
    with ExitStack() as ctx:
        sb = ctx.enter_context(tc.tile_pool(name="sb", bufs=1))
        ps = ctx.enter_context(tc.psum_pool(name="ps", bufs=1))

        def tile(name, shape, dtype):
            return sb.tile(shape, dtype, name=name, align_bytes=64)

        tok_list = sb.tile([P, SLOTS // 16], U16, name="tok_list")
        gate_list = sb.tile([P, SLOTS // 16], U16, name="gate_list")
        tab_w = tile("tab_w", [P, T], U16)
        key_w = tile("key_w", [P, T], U16)
        tab_s = tile("tab_s", [P, T], U8)
        key_s = tile("key_s", [P, T], U8)
        window = tile("window", [P, T], F32)
        warm = tile("warm", [P, 1], F32)
        warm_out = tile("warm_out", [P, 1], F32)

        nc.vector.memset(tab_s[:].bitcast(I32), 0)
        nc.vector.memset(warm[:], 0.0)
        nc.vector.memset(key_s[:].bitcast(I32), 0)
        nc.vector.memset(window[:], 0.0)

        def load_scales(queue, dst, src):
            rows = src[0].rearrange("(g f) c -> f g c", f=4)
            for f in range(4):
                queue.dma_start(out=dst[f:P:32, :].bitcast(I32), in_=rows[f].bitcast(I32))

        def load_rows(name, src, c0, c1):
            raw = tile(name, [P, PACK, c1 - c0], F32)
            nc.sync.dma_start(out=raw[:], in_=src.rearrange("(p t) c -> p t c", t=PACK)[:, :, c0:c1])
            return raw

        gate_rows = gtab.rearrange("(p j) u -> j p u", j=PACK)

        def load_gates(j):
            g = tile("gates%d" % j, [P, U], F32)
            nc.sync.dma_start(out=g[:], in_=gate_rows[j])
            return g

        nc.scalar.activation(warm_out[:], warm[:], ACT.Sigmoid)
        nc.sync.dma_start(tok_list[:], offs)
        nc.sync.dma_start(out=tab_w[:].bitcast(I32), in_=tab_words[0].bitcast(I32))
        load_scales(nc.sync, tab_s, tab_scales)
        w_raw = [load_rows("w_raw0", w1, 0, R // 2)]
        gates = [load_gates(0)]
        nc.sync.dma_start(gate_list[:], offs2)
        load_scales(nc.sync, key_s, keys_scales)
        w_raw.append(load_rows("w_raw1", w1, R // 2, R))
        gates.append(load_gates(1))
        nc.sync.dma_start(out=key_w[:].bitcast(I32), in_=keys_words[0].bitcast(I32))
        hsc_t = tile("hsc_t", [P, PACK], F32)
        nc.sync.dma_start(out=hsc_t[:], in_=hsc.rearrange("(p j) o -> p (j o)", j=PACK))
        gates.append(load_gates(2))
        q2_raw = load_rows("q2_raw", query2, 0, Q)
        gates.append(load_gates(3))
        q_raw = load_rows("q_raw", query, 0, Q)
        go_raw = load_rows("go_raw", gout, 0, Q)
        old_t = tile("old_t", [P, T], F32)
        nc.sync.dma_start(out=old_t[:], in_=old)

        def gather(name, src, dtype):
            dst = tile(name, [P, SLOTS], dtype)
            nc.vector.tensor_copy(dst[:], src[:].indirect(tok_list[:]))
            return dst

        def quantise(name, src, words):
            codes = tile(name + "_codes", [P, words], U32)
            scales = tile(name + "_scales", [P, words], U8)
            nc.vector.quantize_mx(out=codes[:].bitcast(FP8X4), scales=scales[:], in_=src)
            return codes, scales

        def weave(copy, dst, raw):
            copy(out=dst.rearrange("p (c t) -> p c t", t=PACK), in_=raw.rearrange("p t c -> p c t"))
            return dst

        def gate(j):
            hg = tile("hg%d" % j, [P, SLOTS], F32)
            nc.scalar.activation(hg[:], gates[j][:].indirect(gate_list[:]), ACT.Sigmoid)
            return hg

        tab_wg = gather("tab_wg", tab_w, U16)
        tab_sg = gather("tab_sg", tab_s, U8)
        key_sg = gather("key_sg", key_s, U8)

        w_bf = tile("w_bf", [P, R * PACK], BF16)
        w_view = w_bf[:].rearrange("p (j m t) -> p m j t", j=PACK, t=PACK)
        for h, copy in enumerate((nc.scalar.copy, nc.vector.tensor_copy)):
            copy(out=w_view[:, h * 64:(h + 1) * 64], in_=w_raw[h][:].rearrange("p t (m j) -> p m j t", j=PACK))
        w_codes, w_scales = quantise("w", w_bf[:], R)
        zh = []
        for j in range(PACK):
            bank = ps.tile([P, SLOTS], F32, name="zh%d" % j)
            nc.tensor.matmul_mx(out=bank[:], lhsT=w_codes[:, j * P:(j + 1) * P].bitcast(FP8X4),
                                lhsT_scale=w_scales[:, j * P:(j + 1) * P],
                                rhs=tab_wg[:].bitcast(FP4X4), rhs_scale=tab_sg[:], start=True, stop=True)
            zh.append(bank)
        hg = [gate(0)]

        planes = tile("planes", [P, PACK, SLOTS], BF16)

        def hidden(j):
            nc.vector.scalar_tensor_tensor(out=planes[:, j, :], in0=zh[j][:], scalar=hsc_t[:, j:j + 1], in1=hg[j][:],
                                           op0=ALU.mult, op1=ALU.mult)

        def score(name, bf, key_wg):
            codes, scales = quantise(name, bf, Q)
            bank = ps.tile([P, SLOTS], F32, name=name + "_ps")
            nc.tensor.matmul_mx(out=bank[:], lhsT=codes[:].bitcast(FP8X4), lhsT_scale=scales[:],
                                rhs=key_wg[:].bitcast(FP4X4), rhs_scale=key_sg[:], start=True, stop=True)
            return bank

        hg.append(gate(1))
        key_wg = gather("key_wg", key_w, U16)
        hidden(0)
        hg.append(gate(2))
        q2_bf = weave(nc.vector.tensor_copy, planes[:, 2, :], q2_raw[:])
        hidden(1)
        b_ps = score("b", q2_bf, key_wg)
        hg.append(gate(3))
        hidden(2)
        q_bf = weave(nc.vector.tensor_copy, planes[:, 3, :], q_raw[:])
        go_bf = weave(nc.vector.tensor_copy, tile("go_bf", [P, Q * PACK], BF16)[:], go_raw[:])
        a_ps = score("a", q_bf, key_wg)
        sig_b = tile("gates3", [P, SLOTS], F32)
        nc.scalar.activation(sig_b[:], b_ps[:], ACT.Sigmoid)
        hidden(3)
        neg_max = tile("neg_max", [P, 1], F32)
        nc.vector.tensor_reduce(out=neg_max[:], in_=a_ps[:], axis=AX.X, op=ALU.max, negate=True)
        nc.scalar.activation(warm_out[:], hg[3][:, 0:1], ACT.Exp, bias=sig_b[:, 0:1])
        go_codes, go_scales = quantise("go", go_bf, Q)
        e = tile("e", [P, SLOTS], F32)
        nc.scalar.activation(e[:], a_ps[:], ACT.Exp, bias=neg_max[:])

        woven = [weave(nc.vector.tensor_copy, tile("woven%d" % h, [P, HALF * PACK], BF16)[:], planes[:, :, h * HALF:(h + 1) * HALF]) for h in range(2)]
        c0 = ps.tile([P, SLOTS], F32, name="c0")

        def read_grad(h):
            codes, scales = quantise("hs%d" % h, woven[h], HALF)
            nc.tensor.matmul_mx(out=c0[:, h * HALF:(h + 1) * HALF], lhsT=go_codes[:].bitcast(FP8X4),
                                lhsT_scale=go_scales[:], rhs=codes[:].bitcast(FP8X4), rhs_scale=scales[:],
                                start=True, stop=True)

        read_grad(0)
        p = tile("woven0", [P, SLOTS], F32)
        z = tile("z", [P, 1], F32)
        nc.vector.scalar_tensor_tensor(out=p[:], in0=e[:], scalar=1.0, in1=sig_b[:], op0=ALU.mult, op1=ALU.mult,
                                       accum_out=z[:])
        read_grad(1)
        rz = tile("rz", [P, 1], F32)
        nc.vector.reciprocal(rz[:], z[:])
        rz512 = tile("rz512", [P, 1], F32)
        neg_rz = tile("neg_rz", [P, 1], F32)
        nc.vector.tensor_scalar(out=rz512[:], in0=rz[:], scalar1=512.0, scalar2=None, op0=ALU.mult)
        nc.vector.tensor_scalar(out=neg_rz[:], in0=rz[:], scalar1=-1.0, scalar2=None, op0=ALU.mult)
        direct = tile("direct", [P, SLOTS], F32)
        total = tile("total", [P, 1], F32)
        nc.vector.scalar_tensor_tensor(out=direct[:], in0=c0[:], scalar=rz512[:], in1=p[:], op0=ALU.mult,
                                       op1=ALU.mult, accum_out=total[:])
        via_z = tile("via_z", [P, SLOTS], F32)
        nc.vector.tensor_scalar(out=via_z[:], in0=p[:], scalar1=total[:], scalar2=neg_rz[:], op0=ALU.mult,
                                op1=ALU.mult)
        nc.vector.tensor_tensor(window[:].indirect(tok_list[:]), direct[:], via_z[:], ALU.add)

        for c0_, c1_ in zip(OUT_CUTS[:-1], OUT_CUTS[1:]):
            res = tile("res%d" % c0_, [P, c1_ - c0_], F32)
            nc.vector.tensor_tensor(res[:], old_t[:, c0_:c1_], window[:, c0_:c1_], ALU.add)
            nc.sync.dma_start(out=out[:, c0_:c1_], in_=res[:])
